import numpy as np
import ml_dtypes


def mxq(x, axis, fmt="e4m3"):
    dtype, down = {"e4m3": (ml_dtypes.float8_e4m3fn, 7), "e5m2": (ml_dtypes.float8_e5m2, 14)}[fmt]
    v = np.moveaxis(np.asarray(x, np.float32).astype(ml_dtypes.bfloat16).astype(np.float64), axis, -1)
    blocks = v.reshape(v.shape[:-1] + (-1, 32))
    amax = np.abs(blocks).max(-1, keepdims=True)
    byte = np.maximum(np.where(amax > 0, np.frexp(amax)[1] - 1 + 127, 0) - down, 1)
    scale = np.exp2(byte - 127.0)
    codes = (blocks / scale).astype(np.float32).astype(dtype).astype(np.float64)
    return np.moveaxis((codes * scale).reshape(v.shape), -1, axis)


WIDE = False


def mx_kscale(k):
    if not WIDE:
        return np.ones(k)
    levels = np.array([30, -30])
    if k % 512:
        return np.exp2(np.random.permutation(np.resize(levels, k // 32))).repeat(32)
    a = np.empty((k // 512, 16))
    for p in range(k // 512):
        a[p, :8] = np.random.permutation(np.resize(levels, 8))
        for g in range(8):
            far = levels[np.abs(levels - a[p, g]) >= 10]
            a[p, g + 8] = far[np.random.randint(len(far))]
    return np.exp2(a.ravel()).repeat(32)


def f64(x):
    return np.asarray(x).astype(np.float64)


def striped(idx):
    return np.tile(np.asarray(idx).reshape(-1, 16).T, (8, 1)).astype(np.uint16)


def unstriped(offs):
    return offs[:16].T.reshape(-1).astype(np.int64)


E2M1 = np.array([0.0, 0.5, 1.0, 1.5, 2.0, 3.0, 4.0, 6.0, -0.0, -0.5, -1.0, -1.5, -2.0, -3.0, -4.0, -6.0])


def pack_weight(w, fmt):
    k, n = w.shape
    w = f64(np.asarray(w, np.float32).astype(ml_dtypes.bfloat16)).reshape(k // 32, 32, n)
    amax = np.abs(w).max(1)
    if fmt in ("e4m3", "e5m2"):
        byte = np.frexp(amax)[1] - 1 + 127 - (7 if fmt == "e4m3" else 14)
    else:
        mant, ex = np.frexp(amax / 6.0)
        byte = np.where(mant > 0.5, ex, ex - 1) + 127
    byte = np.clip(np.where(amax > 0, byte, 1), 1, 254)
    scaled = (w * np.exp2(127.0 - byte)[:, None, :]).reshape(k, n).astype(np.float32)
    by_word = np.ascontiguousarray(scaled.reshape(k // 512, 128, 4, n).transpose(0, 1, 3, 2))
    if fmt in ("e4m3", "e5m2"):
        words = by_word.astype(ml_dtypes.float8_e4m3fn if fmt == "e4m3" else ml_dtypes.float8_e5m2).view(np.uint8)
    else:
        c = by_word.astype(ml_dtypes.float4_e2m1fn).view(np.uint8) & 0xF
        words = (c[..., 0::2] | (c[..., 1::2] << 4)).reshape(k // 512, 128, 2 * n)
    return np.ascontiguousarray(words), np.ascontiguousarray(byte.astype(np.uint8).reshape(k // 512, 16, n))


def unpack_weight(words, scales, fmt):
    g, _, n = scales.shape
    words = np.ascontiguousarray(words).reshape(g, 128, n, -1)
    if fmt in ("e4m3", "e5m2"):
        vals = words.view(ml_dtypes.float8_e4m3fn if fmt == "e4m3" else ml_dtypes.float8_e5m2).astype(np.float64)
    else:
        nib = np.empty((g, 128, n, 4), np.uint8)
        nib[..., 0::2] = words & 0xF
        nib[..., 1::2] = words >> 4
        vals = E2M1[nib]
    vals = vals * np.repeat(np.exp2(scales.astype(np.float64) - 127.0), 8, axis=1)[..., None]
    return vals.transpose(0, 1, 3, 2).reshape(g * 512, n)


def sgn(shape):
    return np.random.uniform(0.5, 2.0, shape) * np.where(np.random.standard_normal(shape) < 0, -1.0, 1.0)


K, T, J, R, C, D, O, N, U, E = 512, 1024, 256, 512, 512, 512, 256, 256, 128, 512


def setup_inputs():
    n = np.random.standard_normal
    idx = np.random.permutation(T)[:J]
    idx2 = np.random.permutation(C)[:J]
    idx3 = np.random.permutation(D)[:J]
    idx4 = np.random.permutation(D)[:C]
    idx5 = np.random.permutation(C)[:O]
    idx6 = np.random.permutation(O)[:U]
    idx7 = np.random.permutation(E)[:U]
    fk = mx_kscale(K)
    fr = mx_kscale(R)
    xtp = pack_weight(n((K, T)) / fk[:, None], "e5m2")
    wp = pack_weight(n((K, R)) * 1 / np.sqrt(K) * fk[:, None] * fr, "e2m1")
    w2p = pack_weight(n((K, R)) * 1 / np.sqrt(K) * fk[:, None], "e4m3")
    wbp = pack_weight(n((R, N)) * 1 / np.sqrt(R) / fr[:, None], "e2m1")
    return {
        "xt_words": xtp[0],
        "xt_scales": xtp[1],
        "w_words": wp[0],
        "w_scales": wp[1],
        "w2_words": w2p[0],
        "w2_scales": w2p[1],
        "wb_words": wbp[0],
        "wb_scales": wbp[1],
        "so": (sgn((N, 1))).astype(np.float32),
        "offs": striped(idx),
        "offs2": striped(idx2),
        "offs3": striped(idx3),
        "offs4": striped(idx4),
        "offs5": striped(idx5),
        "offs6": striped(idx6),
        "offs7": striped(idx7),
    }


def reference(xt_words, xt_scales, w_words, w_scales, w2_words, w2_scales, wb_words, wb_scales, so, offs, offs2, offs3, offs4, offs5, offs6, offs7):
    idx = unstriped(offs)
    idx2 = unstriped(offs2)
    idx3 = unstriped(offs3)
    idx4 = unstriped(offs4)
    idx5 = unstriped(offs5)
    idx6 = unstriped(offs6)
    idx7 = unstriped(offs7)
    xtu = unpack_weight(xt_words, xt_scales, "e5m2")
    wu = unpack_weight(w_words, w_scales, "e2m1")
    w2u = unpack_weight(w2_words, w2_scales, "e4m3")
    wbu = unpack_weight(wb_words, wb_scales, "e2m1")
    xtidxg = xtu[:, idx]
    a = wu.T @ xtidxg
    b = w2u.T @ xtidxg
    lb = b[:, 0:1]
    la = a[:, 0:1]
    pw = np.zeros((R, C))
    pw[:, idx2] = a
    pv = np.zeros((R, D))
    pv[:, idx3] = b
    pg = np.maximum(pw, pv[:, idx4] * la)
    hid = pg[:, idx5] * lb
    hidq = mxq(hid, 0, "e4m3")
    p = wbu.T @ hidq
    m0 = p[:, idx6] * f64(so)
    y = np.zeros((N, E))
    y[:, idx7] = m0
    return y

from contextlib import ExitStack

import concourse.mybir as mybir

K, T, J, R, C, D, O, N, U, E = 512, 1024, 256, 512, 512, 512, 256, 256, 128, 512
FLOPS = 2 * K * R * J * 2 + 2 * R * N * O

F32 = mybir.dt.float32
BF16 = mybir.dt.bfloat16
I32 = mybir.dt.int32
U32 = mybir.dt.uint32
U16 = mybir.dt.uint16
U8 = mybir.dt.uint8
E4M3 = mybir.dt.float8_e4m3fn_x4
E5M2 = mybir.dt.float8_e5m2_x4
E2M1 = mybir.dt.float4_e2m1fn_x4
COPY = mybir.ActivationFunctionType.Copy
MAX = mybir.AluOpType.max

P = 128
PACK = 4
QUAD = 32
LIST = 16
SHARE = 128


def tile_list_leadcrossboards_twow_one_postedout_kernel(
    tc, xt_words, xt_scales, w_words, w_scales, w2_words, w2_scales, wb_words, wb_scales, so,
    offs, offs2, offs3, offs4, offs5, offs6, offs7, out,
):
    nc = tc.nc
    with ExitStack() as ctx:
        sb = ctx.enter_context(tc.tile_pool(name="sb", bufs=1))
        ps = ctx.enter_context(tc.psum_pool(name="ps", bufs=1))

        def list_tile(src, name):
            tile = sb.tile([P, src.shape[1]], U16, name=name)
            nc.sync.dma_start(tile[:], src)
            return tile

        def staged_rows(scales):
            return scales[0].bitcast(I32).rearrange("(q r) c -> r q c", r=PACK)

        x_stage = sb.tile([PACK, PACK, T // 4], I32, name="x_stage")
        nc.sync.dma_start(x_stage[:], staged_rows(xt_scales))
        w_stage = sb.tile([PACK, PACK, 2, R // 4], I32, name="w_stage")
        nc.scalar.dma_start(w_stage[:, :, 0, :], staged_rows(w2_scales))
        nc.scalar.dma_start(w_stage[:, :, 1, :], staged_rows(w_scales))
        tokens = list_tile(offs, "tokens")
        w2_raw = sb.tile([P, R], U32, name="w2_raw")
        nc.scalar.dma_start(w2_raw[:].bitcast(I32), w2_words[0].rearrange("p n t -> p (n t)").bitcast(I32))
        x_words = sb.tile([P, T], U32, name="x_words")
        nc.sync.dma_start(x_words[:].bitcast(I32), xt_words[0].rearrange("p n t -> p (n t)").bitcast(I32))
        w_raw = sb.tile([P, R], U16, name="w_raw")
        nc.scalar.dma_start(w_raw[:].bitcast(I32), w_words[0].bitcast(I32))
        second_cols = list_tile(offs3, "second_cols")
        first_cols = list_tile(offs2, "first_cols")
        cross_cols = list_tile(offs4, "cross_cols")
        read_cols = list_tile(offs5, "read_cols")

        x_plane = sb.tile([P, T], U8, name="x_plane")
        nc.vector.memset(x_plane[:].bitcast(I32), 0)
        w_plane = sb.tile([P, 2, R], U8, name="w_plane")
        w_plane_words = w_plane[:].rearrange("p w n -> p (w n)").bitcast(I32)
        nc.vector.memset(w_plane_words, 0)
        for q in range(PACK):
            nc.vector.tensor_copy(x_plane[QUAD * q : QUAD * q + PACK, :].bitcast(I32), x_stage[:, q, :])
        for q in range(PACK):
            nc.vector.tensor_copy(
                w_plane_words[QUAD * q : QUAD * q + PACK, :], w_stage[:, q, :, :].rearrange("r w c -> r (w c)")
            )
        xg_plane = sb.tile([P, J], U8, name="xg_plane", align_bytes=64)
        nc.vector.tensor_copy(xg_plane[:], x_plane[:].indirect(tokens[:]))
        dealt_plane = sb.tile([P, 2, PACK, P], U8, name="dealt_plane", align_bytes=64)
        nc.vector.tensor_copy(dealt_plane[:], w_plane[:].rearrange("p w (m t) -> p w t m", t=PACK))
        xg_words = sb.tile([P, J], U32, name="xg_words", align_bytes=64)
        nc.vector.tensor_copy(xg_words[:], x_words[:].indirect(tokens[:]))

        w2_dealt = sb.tile([P, PACK, P], U32, name="w2_dealt", align_bytes=64)
        nc.scalar.copy(
            w2_dealt[:].rearrange("p t (g i) -> p g t i", i=4),
            w2_raw[:].rearrange("p (g i t) -> p g t i", i=4, t=PACK),
        )
        w_dealt = sb.tile([P, PACK, P], U16, name="w_dealt", align_bytes=64)
        nc.scalar.copy(w_dealt[:], w_raw[:].rearrange("p (m t) -> p t m", t=PACK))

        wb_codes = sb.tile([P, N], U16, name="wb_codes", align_bytes=64)
        nc.sync.dma_start(wb_codes[:].bitcast(I32), wb_words[0].bitcast(I32))
        wb_plane = sb.tile([P, N], U8, name="wb_plane", align_bytes=64)
        nc.vector.memset(wb_plane[:].bitcast(I32), 0)
        for q in range(PACK):
            nc.sync.dma_start(
                wb_plane[QUAD * q : QUAD * q + PACK, :].bitcast(I32),
                wb_scales[0, PACK * q : PACK * (q + 1), :].bitcast(I32),
            )
        weights = []
        for h in range(N // P):
            weight = sb.tile([P, 1], F32, name="weight%d" % h)
            nc.sync.dma_start(weight[:], so[P * h : P * (h + 1), :])
            weights.append(weight)
        end_cols = list_tile(offs6, "end_cols")
        page_cols = list_tile(offs7, "page_cols")

        pv, pw = [], []
        for t in range(2):
            pv.append(sb.tile([P, 2 * D], F32, name="pv%d" % t))
            pw.append(sb.tile([P, C], F32, name="pw%d" % t))
            nc.vector.memset(pv[t][:, :D], 0.0)
            nc.vector.memset(pw[t][:], 0.0)
        pv, pw = pv * 2, pw * 2

        def products(t, b_out, a_out):
            nc.tensor.matmul_mx(out=b_out, lhsT=w2_dealt[:, t, :].bitcast(E4M3), lhsT_scale=dealt_plane[:, 0, t, :],
                                rhs=xg_words[:].bitcast(E5M2), rhs_scale=xg_plane[:], start=True, stop=True)
            nc.tensor.matmul_mx(out=a_out, lhsT=w_dealt[:, t, :].bitcast(E2M1), lhsT_scale=dealt_plane[:, 1, t, :],
                                rhs=xg_words[:].bitcast(E5M2), rhs_scale=xg_plane[:], start=True, stop=True)

        b0_bank = ps.tile([P, J], F32, name="b0_bank")
        a0_bank = ps.tile([P, J], F32, name="a0_bank")
        products(0, b0_bank[:], a0_bank[:])
        banks = [None]
        for t in range(1, PACK):
            banks.append(ps.tile([P, 2, J], F32, name="bank%d" % t))
            products(t, banks[t][:, 0, :], banks[t][:, 1, :])

        b0 = sb.tile([P, J], F32, name="b0")
        a0 = sb.tile([P, J], F32, name="a0")
        both = [None] + [sb.tile([P, 2, J], F32, name="both%d" % t) for t in range(1, PACK)]
        b = [b0[:]] + [both[t][:, 0, :] for t in range(1, PACK)]
        a = [a0[:]] + [both[t][:, 1, :] for t in range(1, PACK)]
        crossed = [sb.tile([P, C], F32, name="crossed%d" % t) for t in range(PACK)]
        pg = [sb.tile([P, C], F32, name="pg%d" % t) for t in range(PACK)]
        hid = sb.tile([P, PACK, O], F32, name="hid")

        def leave(t):
            nc.scalar.copy(both[t][:], banks[t][:])

        def put_b(t):
            nc.vector.tensor_copy(pv[t][:].indirect(second_cols[:]), b[t])

        def put_a_scalar(t):
            nc.scalar.activation(pw[t][:].indirect(first_cols[:, :SHARE // LIST]), a[t][:, :SHARE], COPY)

        def put_a_vector(t):
            nc.vector.tensor_copy(pw[t][:].indirect(first_cols[:, SHARE // LIST :]), a[t][:, SHARE:])

        def cross(t, parts):
            width = C // parts
            for s in range(parts):
                nc.scalar.activation(
                    crossed[t][:, s * width : (s + 1) * width],
                    pv[t][:].indirect(cross_cols[:, s * width // LIST : (s + 1) * width // LIST]),
                    COPY, scale=a[t][:, 0:1],
                )

        def keep(t, parts):
            width = C // parts
            for s in range(parts):
                cols = slice(s * width, (s + 1) * width)
                nc.vector.tensor_tensor(pg[t][:, cols], pw[t][:, cols], crossed[t][:, cols], MAX)

        def read(t, parts):
            width = O // parts
            for s in range(parts):
                nc.scalar.activation(
                    hid[:, t, s * width : (s + 1) * width],
                    pg[t][:].indirect(read_cols[:, s * width // LIST : (s + 1) * width // LIST]),
                    COPY, scale=b[t][:, 0:1],
                )

        pages = []
        for h in range(N // P):
            pages.append(sb.tile([P, E], F32, name="page%d" % h))
            nc.vector.memset(pages[h][:], 0.0)

        nc.vector.tensor_copy(b[0], b0_bank[:])
        nc.scalar.activation(a[0], a0_bank[:], COPY)
        for t in range(PACK):
            put_b(t)
            if t > 0:
                keep(t - 1, 1)
            put_a_scalar(t)
            put_a_vector(t)
            if t + 1 < PACK:
                leave(t + 1)
            cross(t, 2 if t == PACK - 1 else 1)
            if t > 0:
                read(t - 1, 1)
        keep(PACK - 1, 2)
        read(PACK - 1, 2)

        grouped = sb.tile([P, O, PACK], BF16, name="grouped", align_bytes=64)
        hid_codes = sb.tile([P, O], U32, name="hid_codes", align_bytes=64)
        hid_plane = sb.tile([P, O], U8, name="hid_plane", align_bytes=64)
        halves = [slice(0, O // 2), slice(O // 2, O)]
        for reads in halves:
            nc.vector.tensor_copy(
                grouped[:, reads, :].rearrange("p (g i) t -> p g t i", i=4),
                hid[:, :, reads].rearrange("p t (g i) -> p g t i", i=4),
            )
        for reads in halves:
            nc.vector.quantize_mx(out=hid_codes[:, reads].bitcast(E4M3), scales=hid_plane[:, reads],
                                  in_=grouped[:, reads, :].rearrange("p o t -> p (o t)"))

        p_banks = [ps.tile([P, O], F32, name="p_bank%d" % h) for h in range(N // P)]
        for reads in halves:
            for h in range(N // P):
                cols = slice(P * h, P * (h + 1))
                nc.tensor.matmul_mx(out=p_banks[h][:, reads], lhsT=wb_codes[:, cols].bitcast(E2M1),
                                    lhsT_scale=wb_plane[:, cols], rhs=hid_codes[:, reads].bitcast(E4M3),
                                    rhs_scale=hid_plane[:, reads], start=True, stop=True)

        results, ends = [], []
        for h in range(N // P):
            bank = p_banks[h]
            result = sb.tile([P, O], F32, name="result%d" % h)
            if h == 0:
                nc.scalar.copy(result[:], bank[:])
            else:
                nc.vector.tensor_copy(result[:], bank[:])
            results.append(result)
        for h in range(N // P):
            end = sb.tile([P, U], F32, name="end%d" % h)
            nc.scalar.activation(end[:], results[h][:].indirect(end_cols[:]), COPY, scale=weights[h][:])
            ends.append(end)
        nc.vector.tensor_copy(pages[0][:].indirect(page_cols[:]), ends[0][:])
        nc.sync.dma_start(out[0:P, :], pages[0][:])
        nc.scalar.activation(pages[1][:].indirect(page_cols[:]), ends[1][:], COPY)
        nc.scalar.dma_start(out[P : 2 * P, :], pages[1][:])
